import numpy as np
import ml_dtypes


def mxq(x, axis, fmt="e4m3"):
    dtype, down = {"e4m3": (ml_dtypes.float8_e4m3fn, 7), "e5m2": (ml_dtypes.float8_e5m2, 14)}[fmt]
    v = np.moveaxis(np.asarray(x, np.float32).astype(ml_dtypes.bfloat16).astype(np.float64), axis, -1)
    blocks = v.reshape(v.shape[:-1] + (-1, 32))
    amax = np.abs(blocks).max(-1, keepdims=True)
    byte = np.maximum(np.where(amax > 0, np.frexp(amax)[1] - 1 + 127, 0) - down, 1)
    scale = np.exp2(byte - 127.0)
    codes = (blocks / scale).astype(np.float32).astype(dtype).astype(np.float64)
    return np.moveaxis((codes * scale).reshape(v.shape), -1, axis)


WIDE = False


def mx_kscale(k):
    if not WIDE:
        return np.ones(k)
    levels = np.array([10, -10, 5, -5, 0])
    if k % 512:
        return np.exp2(np.random.permutation(np.resize(levels, k // 32))).repeat(32)
    a = np.empty((k // 512, 16))
    for p in range(k // 512):
        a[p, :8] = np.random.permutation(np.resize(levels, 8))
        for g in range(8):
            far = levels[np.abs(levels - a[p, g]) >= 10]
            a[p, g + 8] = far[np.random.randint(len(far))]
    return np.exp2(a.ravel()).repeat(32)


def f64(x):
    return np.asarray(x).astype(np.float64)


def striped(idx):
    return np.tile(np.asarray(idx).reshape(-1, 16).T, (8, 1)).astype(np.uint16)


def unstriped(offs):
    return offs[:16].T.reshape(-1).astype(np.int64)


def striped8(idx):
    return np.asarray(idx).reshape(8, -1, 16).transpose(0, 2, 1).reshape(128, -1).astype(np.uint16)


def unstriped8(offs):
    return offs.reshape(8, 16, -1).transpose(0, 2, 1).reshape(8, -1).astype(np.int64)


def pick8(x, idx, run):
    r = np.arange(len(x))
    return x[r[:, None], idx[r % (8 * run) // run]]


E2M1 = np.array([0.0, 0.5, 1.0, 1.5, 2.0, 3.0, 4.0, 6.0, -0.0, -0.5, -1.0, -1.5, -2.0, -3.0, -4.0, -6.0])


def pack_weight(w, fmt):
    k, n = w.shape
    w = f64(np.asarray(w, np.float32).astype(ml_dtypes.bfloat16)).reshape(k // 32, 32, n)
    amax = np.abs(w).max(1)
    if fmt == "e4m3":
        byte = np.frexp(amax)[1] - 1 + 127 - 7
    else:
        mant, ex = np.frexp(amax / 6.0)
        byte = np.where(mant > 0.5, ex, ex - 1) + 127
    byte = np.clip(np.where(amax > 0, byte, 1), 1, 254)
    scaled = (w * np.exp2(127.0 - byte)[:, None, :]).reshape(k, n).astype(np.float32)
    by_word = np.ascontiguousarray(scaled.reshape(k // 512, 128, 4, n).transpose(0, 1, 3, 2))
    if fmt == "e4m3":
        words = by_word.astype(ml_dtypes.float8_e4m3fn).view(np.uint8)
    else:
        c = by_word.astype(ml_dtypes.float4_e2m1fn).view(np.uint8) & 0xF
        words = (c[..., 0::2] | (c[..., 1::2] << 4)).reshape(k // 512, 128, 2 * n)
    return np.ascontiguousarray(words), np.ascontiguousarray(byte.astype(np.uint8).reshape(k // 512, 16, n))


def unpack_weight(words, scales, fmt):
    g, _, n = scales.shape
    words = np.ascontiguousarray(words).reshape(g, 128, n, -1)
    if fmt == "e4m3":
        vals = words.view(ml_dtypes.float8_e4m3fn).astype(np.float64)
    else:
        nib = np.empty((g, 128, n, 4), np.uint8)
        nib[..., 0::2] = words & 0xF
        nib[..., 1::2] = words >> 4
        vals = E2M1[nib]
    vals = vals * np.repeat(np.exp2(scales.astype(np.float64) - 127.0), 8, axis=1)[..., None]
    return vals.transpose(0, 1, 3, 2).reshape(g * 512, n)


def bf(x):
    return np.asarray(x, np.float32).astype(ml_dtypes.bfloat16)


def planes(Y):
    r, m = Y.shape
    b = f64(bf(Y)).reshape(r // 32, 32, m)
    amax = np.abs(b).max(1)
    byte = np.clip(np.where(amax > 0, np.frexp(amax)[1] - 1 + 127 - 7, 1), 1, 254)
    codes = (b * np.exp2(127.0 - byte)[:, None, :]).reshape(r, m).astype(np.float32).astype(ml_dtypes.float8_e4m3fn).view(np.uint8)
    words = codes.reshape(r // 512, 128, 4, m).transpose(0, 1, 3, 2)
    return np.ascontiguousarray(words), np.ascontiguousarray(byte.astype(np.uint8).reshape(r // 512, 16, m))


K, R, F, T, J, U = 512, 512, 512, 2048, 256, 512


def setup_inputs():
    n = np.random.standard_normal
    idx = np.random.permutation(T)[:J]
    idx2 = np.stack([np.random.permutation(U)[:J] for _ in range(8)])
    idx3 = np.stack([np.random.permutation(U)[:J] for _ in range(8)])
    fk = mx_kscale(K)
    fr = mx_kscale(R)
    tabp = pack_weight(n((K, T)) / fk[:, None], "e4m3")
    return {
        "tab_words": tabp[0],
        "tab_scales": tabp[1],
        "w1": (n((K, R)) * 1 / np.sqrt(K) * fk[:, None]).astype(np.float32),
        "gain": (np.random.uniform(0.5, 1.5, (R, 1))).astype(np.float32),
        "ground": (n((R, U)) * 0.7).astype(np.float32),
        "rs": (np.random.uniform(0.5, 2.0, (R, 1)) * fr[:, None]).astype(np.float32),
        "wor": (n((R, F)) * 1 / np.sqrt(R) / fr[:, None]).astype(np.float32),
        "res": (n((F, U)) * 0.5).astype(np.float32),
        "offs": striped(idx),
        "offs2": striped8(idx2),
        "offs3": striped8(idx3),
    }


def reference(tab_words, tab_scales, w1, gain, ground, rs, wor, res, offs, offs2, offs3):
    idx = unstriped(offs)
    idx2 = unstriped8(offs2)
    idx3 = unstriped8(offs3)
    tabu = unpack_weight(tab_words, tab_scales, "e4m3")
    w1q = mxq(f64(w1), 0, "e4m3")
    tabidxg = tabu[:, idx]
    a = w1q.T @ tabidxg
    h0 = np.tanh(a)
    h1 = h0 * f64(gain)
    pa = np.zeros((R, U))
    pa[np.arange(R)[:, None], idx2[np.arange(R) % 512 // 64]] = h1
    pb = np.zeros((R, U))
    pb[np.arange(R)[:, None], idx3[np.arange(R) % 512 // 64]] = a
    u1 = (pa + f64(ground)) / (np.square(pb) + 1.0)
    fo1 = u1 * f64(rs)
    worq = mxq(f64(wor), 0, "e4m3")
    fo1q = mxq(fo1, 0, "e4m3")
    yo = worq.T @ fo1q
    y = yo + f64(res)
    words, scales = planes(y)
    return y, words, scales

@@ -1,0 +1,236 @@
+from contextlib import ExitStack
+
+import concourse.mybir as mybir
+from concourse.masks import make_identity
+
+K, R, F, T, J, U = 512, 512, 512, 2048, 256, 512
+FLOPS = 2 * K * R * J + 2 * R * F * U
+
+F32 = mybir.dt.float32
+BF16 = mybir.dt.bfloat16
+I32 = mybir.dt.int32
+U32 = mybir.dt.uint32
+U16 = mybir.dt.uint16
+U8 = mybir.dt.uint8
+FP8X4 = mybir.dt.float8_e4m3fn_x4
+ACT = mybir.ActivationFunctionType
+MULT = mybir.AluOpType.mult
+ADD = mybir.AluOpType.add
+
+P = 128
+PACK = 4
+QUADS = 4
+CHUNK = 128
+
+
+def dealt_views(grouped, raw, m0, m1):
+    dst = grouped[:].rearrange("p t m j -> p m j t")[:, m0:m1]
+    src = raw[:].rearrange("p j (m t) -> p m j t", t=PACK)[:, m0:m1]
+    return dst, src
+
+
+def woven_views(woven, planar):
+    dst = woven.rearrange("p (c i) t -> p c t i", i=PACK)
+    src = planar.rearrange("p t (c i) -> p c t i", i=PACK)
+    return dst, src
+
+
+def tile_attend_chpageratio_pl_kernel(
+    tc, tab_words, tab_scales, w1, gain, ground, rs, wor, res, offs, offs2, offs3, out_0, out_1, out_2
+):
+    nc = tc.nc
+    with ExitStack() as ctx:
+        lists = ctx.enter_context(tc.tile_pool(name="lists", bufs=1))
+        keep = ctx.enter_context(tc.tile_pool(name="keep", bufs=1))
+        psum = ctx.enter_context(tc.psum_pool(name="psum", bufs=1))
+
+        def by_rows(dram):
+            return dram.rearrange("(p t) c -> p t c", t=PACK)
+
+        offs_sb = lists.tile([P, J // 16], U16, name="offs_sb")
+        offs2_sb = lists.tile([P, J // 16], U16, name="offs2_sb")
+        offs3_sb = lists.tile([P, J // 16], U16, name="offs3_sb")
+        tab_bytes = keep.tile([P, T], U8, name="tab_bytes", align_bytes=64)
+        nc.vector.memset(tab_bytes[:].bitcast(I32), 0)
+        warm = keep.tile([P, 1], F32, name="warm")
+        warm_out = keep.tile([P, 1], F32, name="warm_out")
+        nc.vector.memset(warm[:], 0.0)
+        nc.sync.dma_start(offs_sb[:], offs)
+        w1_raw = keep.tile([P, PACK, R], F32, name="w1_raw", tag="slot_a", align_bytes=64)
+        nc.sync.dma_start(w1_raw[:], by_rows(w1))
+        for q in range(QUADS):
+            nc.scalar.dma_start(
+                tab_bytes[32 * q : 32 * q + 4, :].bitcast(I32), tab_scales[0, 4 * q : 4 * q + 4, :].bitcast(I32)
+            )
+        nc.scalar.activation(warm_out[:], warm[:], ACT.Tanh)
+        tab_sb = keep.tile([P, T], I32, name="tab_sb", align_bytes=64)
+        nc.sync.dma_start(tab_sb[:], tab_words[0].rearrange("p c t -> p (c t)").bitcast(I32))
+        nc.sync.dma_start(offs2_sb[:], offs2)
+        nc.sync.dma_start(offs3_sb[:], offs3)
+        gain_sb = keep.tile([P, PACK], F32, name="gain_sb")
+        rs_sb = keep.tile([P, PACK], F32, name="rs_sb")
+        nc.gpsimd.dma_start(gain_sb[:], gain.rearrange("(p t) o -> p (t o)", t=PACK))
+        nc.gpsimd.dma_start(rs_sb[:], rs.rearrange("(p t) o -> p (t o)", t=PACK))
+
+        ident = keep.tile([P, P], F32, name="ident")
+        make_identity(nc, ident[:])
+        page_a = [keep.tile([P, U], F32, name="page_a%d" % t) for t in range(PACK)]
+        page_q = [keep.tile([P, U], F32, name="page_q%d" % t) for t in range(PACK)]
+        for t in range(PACK):
+            nc.vector.memset(page_a[t][:], 0.0)
+        for t in range(PACK):
+            nc.vector.memset(page_q[t][:], 1.0)
+
+        gain_wide = [keep.tile([P, J], F32, name="gain_wide%d" % t) for t in range(PACK)]
+        for t in range(PACK):
+            nc.scalar.copy(gain_wide[t][:], gain_sb[:, t : t + 1].to_broadcast([P, J]))
+
+        w1_bf = keep.tile([P, PACK, P, PACK], BF16, name="w1_bf", tag="slot_b", align_bytes=64)
+        dst, src = dealt_views(w1_bf, w1_raw, 0, 48)
+        nc.scalar.copy(dst, src)
+        dst, src = dealt_views(w1_bf, w1_raw, 48, P)
+        nc.vector.tensor_copy(dst, src)
+        w1_codes = keep.tile([P, R], U32, name="w1_codes", tag="slot_c", align_bytes=64)
+        w1_scales = keep.tile([P, R], U8, name="w1_scales", align_bytes=64)
+        picked_bytes = keep.tile([P, J], U8, name="picked_bytes", align_bytes=64)
+        nc.vector.tensor_copy(picked_bytes[:], tab_bytes[:].indirect(offs_sb[:]))
+        nc.vector.quantize_mx(
+            out=w1_codes[:].bitcast(FP8X4), scales=w1_scales[:], in_=w1_bf[:].rearrange("p t m j -> p (t m j)")
+        )
+        picked_words = keep.tile([P, J], U32, name="picked_words", align_bytes=64)
+        nc.vector.tensor_copy(picked_words[:], tab_sb[:].bitcast(U32).indirect(offs_sb[:]))
+
+        a_banks = [psum.tile([P, J], F32, name="a_bank%d" % t, tag="bank%d" % t) for t in range(PACK)]
+        for t in range(PACK):
+            cols = slice(t * P, (t + 1) * P)
+            nc.tensor.matmul_mx(
+                out=a_banks[t][:],
+                lhsT=w1_codes[:, cols].bitcast(FP8X4),
+                lhsT_scale=w1_scales[:, cols],
+                rhs=picked_words[:].bitcast(FP8X4),
+                rhs_scale=picked_bytes[:],
+                start=True,
+                stop=True,
+            )
+
+        ground_sb = keep.tile([P, PACK, U], F32, name="ground_sb", tag="slot_a", align_bytes=64)
+        nc.sync.dma_start(ground_sb[:], by_rows(ground))
+        wor_raw = keep.tile([P, PACK, F], F32, name="wor_raw", tag="slot_b", align_bytes=64)
+        nc.sync.dma_start(wor_raw[:], by_rows(wor))
+        res_sb = keep.tile([P, PACK, U], F32, name="res_sb", tag="slot_c", align_bytes=64)
+        nc.sync.dma_start(res_sb[:], by_rows(res))
+
+        for t in range(PACK):
+            h0 = keep.tile([P, J], F32, name="h0_%d" % t)
+            nc.scalar.activation(h0[:], a_banks[t][:], ACT.Tanh)
+            nc.vector.tensor_tensor(page_a[t][:].indirect(offs2_sb[:]), h0[:], gain_wide[t][:], MULT)
+        a_sq = [keep.tile([P, J], F32, name="a_sq%d" % t) for t in range(PACK)]
+        for t in range(PACK):
+            nc.scalar.activation(a_sq[t][:], a_banks[t][:], ACT.Square)
+        numer = [psum.tile([P, U], F32, name="numer%d" % t) for t in range(PACK)]
+
+        def add_ground(t):
+            turned = psum.tile([P, PACK, P], F32, name="turned%d" % t, tag="bank%d" % t)
+            for b in range(U // P):
+                cols = slice(b * P, (b + 1) * P)
+                nc.tensor.matmul(
+                    turned[:, b, :], ground_sb[:, t, cols], ident[:], start=True, stop=False, is_transpose=True
+                )
+                nc.tensor.matmul(
+                    turned[:, b, :], page_a[t][:, cols], ident[:], start=False, stop=True, is_transpose=True
+                )
+            turned_sb = keep.tile([P, PACK, P], F32, name="turned_sb%d" % t, tag="root%d" % t)
+            nc.scalar.copy(turned_sb[:], turned[:])
+            for b in range(U // P):
+                nc.tensor.transpose(numer[t][:, b * P : (b + 1) * P], turned_sb[:, b, :], ident[:])
+
+        fo_planar = keep.tile([P, PACK, U], BF16, name="fo_planar")
+        wor_bf = keep.tile([P, PACK, P, PACK], BF16, name="wor_bf", align_bytes=64)
+        wor_codes = keep.tile([P, F], U32, name="wor_codes", align_bytes=64)
+        wor_scales = keep.tile([P, F], U8, name="wor_scales", align_bytes=64)
+
+        def scatter_q(t):
+            root = keep.tile([P, J], F32, name="root%d" % t, tag="root%d" % t)
+            recip = keep.tile([P, J], F32, name="recip%d" % t)
+            nc.scalar.activation(root[:], a_sq[t][:], ACT.Abs_reciprocal_sqrt, bias=1.0)
+            nc.scalar.activation(recip[:], root[:], ACT.Square)
+            nc.vector.tensor_copy(page_q[t][:].indirect(offs3_sb[:]), recip[:])
+
+        def outcome(t, cols):
+            nc.vector.scalar_tensor_tensor(
+                fo_planar[:, t, cols], numer[t][:, cols], rs_sb[:, t : t + 1], page_q[t][:, cols], MULT, MULT
+            )
+
+        def round_wor(m0):
+            dst, src = dealt_views(wor_bf, wor_raw, m0, m0 + 32)
+            nc.scalar.copy(dst, src)
+
+        scatter_q(0)
+        add_ground(0)
+        scatter_q(1)
+        outcome(0, slice(0, U))
+        add_ground(1)
+        round_wor(0)
+        round_wor(32)
+        scatter_q(2)
+        outcome(1, slice(0, U))
+        add_ground(2)
+        round_wor(64)
+        round_wor(96)
+        nc.vector.quantize_mx(
+            out=wor_codes[:].bitcast(FP8X4), scales=wor_scales[:], in_=wor_bf[:].rearrange("p t m j -> p (t m j)")
+        )
+        outcome(2, slice(0, U))
+        scatter_q(3)
+        add_ground(3)
+
+        y_codes = keep.tile([P, U], U32, name="y_codes", align_bytes=64)
+        y_scales = keep.tile([P, U], U8, name="y_scales", align_bytes=64)
+        out_rows = by_rows(out_0)
+        out_words = out_1[0].rearrange("p c t -> p (c t)").bitcast(I32)
+        chunks = [slice(c0, c0 + CHUNK) for c0 in range(0, U, CHUNK)]
+        y_banks = []
+        for c, cols in enumerate(chunks):
+            outcome(PACK - 1, cols)
+        for c, cols in enumerate(chunks):
+            fo_woven = keep.tile([P, CHUNK, PACK], BF16, name="fo_woven%d" % c, align_bytes=64)
+            dst, src = woven_views(fo_woven[:], fo_planar[:, :, cols])
+            nc.scalar.copy(dst, src)
+            fo_codes = keep.tile([P, CHUNK], U32, name="fo_codes%d" % c, align_bytes=64)
+            fo_scales = keep.tile([P, CHUNK], U8, name="fo_scales%d" % c, align_bytes=64)
+            nc.vector.quantize_mx(
+                out=fo_codes[:].bitcast(FP8X4), scales=fo_scales[:], in_=fo_woven[:].rearrange("p u t -> p (u t)")
+            )
+            y_bank = psum.tile([P, PACK, CHUNK], F32, name="y_bank%d" % c, tag="bank%d" % c)
+            y_banks.append(y_bank)
+            for j in range(PACK):
+                wcols = slice(j * P, (j + 1) * P)
+                nc.tensor.matmul_mx(
+                    out=y_bank[:, j, :],
+                    lhsT=wor_codes[:, wcols].bitcast(FP8X4),
+                    lhsT_scale=wor_scales[:, wcols],
+                    rhs=fo_codes[:].bitcast(FP8X4),
+                    rhs_scale=fo_scales[:],
+                    start=True,
+                    stop=True,
+                )
+        for c, cols in enumerate(chunks):
+            y_sb = keep.tile([P, PACK, CHUNK], F32, name="y_sb%d" % c)
+            nc.vector.tensor_tensor(y_sb[:], y_banks[c][:], res_sb[:, :, cols], ADD)
+            nc.sync.dma_start(out_rows[:, :, cols], y_sb[:])
+            y_woven = keep.tile([P, CHUNK, PACK], BF16, name="y_woven%d" % c, align_bytes=64)
+            dst, src = woven_views(y_woven[:], y_sb[:])
+            nc.scalar.copy(dst, src)
+            nc.vector.quantize_mx(
+                out=y_codes[:, cols].bitcast(FP8X4),
+                scales=y_scales[:, cols],
+                in_=y_woven[:].rearrange("p u t -> p (u t)"),
+            )
+            if c % 2 == 1:
+                half = slice(cols.stop - 2 * CHUNK, cols.stop)
+                nc.sync.dma_start(out_words[:, half], y_codes[:, half].bitcast(I32))
+        for q in range(QUADS):
+            queue = nc.scalar if q % 2 == 0 else nc.sync
+            queue.dma_start(
+                out_2[0, 4 * q : 4 * q + 4, :].bitcast(I32), y_scales[32 * q : 32 * q + 4, :].bitcast(I32)
+            )

@@ -1,7 +1,6 @@
 from contextlib import ExitStack
 
 import concourse.mybir as mybir
-from concourse.masks import make_identity
 
 K, R, F, T, J, U = 512, 512, 512, 2048, 256, 512
 FLOPS = 2 * K * R * J + 2 * R * F * U
@@ -56,6 +55,8 @@ def tile_attend_chpageratio_pl_kernel(
         warm_out = keep.tile([P, 1], F32, name="warm_out")
         nc.vector.memset(warm[:], 0.0)
         nc.sync.dma_start(offs_sb[:], offs)
+        gain_sb = keep.tile([P, PACK], F32, name="gain_sb")
+        nc.scalar.dma_start(gain_sb[:], gain.rearrange("(p t) o -> p (t o)", t=PACK))
         w1_raw = keep.tile([P, PACK, R], F32, name="w1_raw", tag="slot_a", align_bytes=64)
         nc.sync.dma_start(w1_raw[:], by_rows(w1))
         for q in range(QUADS):
@@ -67,13 +68,7 @@ def tile_attend_chpageratio_pl_kernel(
         nc.sync.dma_start(tab_sb[:], tab_words[0].rearrange("p c t -> p (c t)").bitcast(I32))
         nc.sync.dma_start(offs2_sb[:], offs2)
         nc.sync.dma_start(offs3_sb[:], offs3)
-        gain_sb = keep.tile([P, PACK], F32, name="gain_sb")
-        rs_sb = keep.tile([P, PACK], F32, name="rs_sb")
-        nc.gpsimd.dma_start(gain_sb[:], gain.rearrange("(p t) o -> p (t o)", t=PACK))
-        nc.gpsimd.dma_start(rs_sb[:], rs.rearrange("(p t) o -> p (t o)", t=PACK))
 
-        ident = keep.tile([P, P], F32, name="ident")
-        make_identity(nc, ident[:])
         page_a = [keep.tile([P, U], F32, name="page_a%d" % t) for t in range(PACK)]
         page_q = [keep.tile([P, U], F32, name="page_q%d" % t) for t in range(PACK)]
         for t in range(PACK):
@@ -81,9 +76,8 @@ def tile_attend_chpageratio_pl_kernel(
         for t in range(PACK):
             nc.vector.memset(page_q[t][:], 1.0)
 
-        gain_wide = [keep.tile([P, J], F32, name="gain_wide%d" % t) for t in range(PACK)]
-        for t in range(PACK):
-            nc.scalar.copy(gain_wide[t][:], gain_sb[:, t : t + 1].to_broadcast([P, J]))
+        gain_wide = keep.tile([P, J], F32, name="gain_wide")
+        nc.scalar.copy(gain_wide[:], gain_sb[:, 0:1].to_broadcast([P, J]))
 
         w1_bf = keep.tile([P, PACK, P, PACK], BF16, name="w1_bf", tag="slot_b", align_bytes=64)
         dst, src = dealt_views(w1_bf, w1_raw, 0, 48)
@@ -91,7 +85,7 @@ def tile_attend_chpageratio_pl_kernel(
         dst, src = dealt_views(w1_bf, w1_raw, 48, P)
         nc.vector.tensor_copy(dst, src)
         w1_codes = keep.tile([P, R], U32, name="w1_codes", tag="slot_c", align_bytes=64)
-        w1_scales = keep.tile([P, R], U8, name="w1_scales", align_bytes=64)
+        w1_scales = keep.tile([P, R], U8, name="w1_scales", tag="slot_d", align_bytes=64)
         picked_bytes = keep.tile([P, J], U8, name="picked_bytes", align_bytes=64)
         nc.vector.tensor_copy(picked_bytes[:], tab_bytes[:].indirect(offs_sb[:]))
         nc.vector.quantize_mx(
@@ -117,84 +111,77 @@ def tile_attend_chpageratio_pl_kernel(
         nc.sync.dma_start(ground_sb[:], by_rows(ground))
         wor_raw = keep.tile([P, PACK, F], F32, name="wor_raw", tag="slot_b", align_bytes=64)
         nc.sync.dma_start(wor_raw[:], by_rows(wor))
+        rs_sb = keep.tile([P, PACK], F32, name="rs_sb", tag="slot_d", align_bytes=64)
+        nc.sync.dma_start(rs_sb[:], rs.rearrange("(p t) o -> p (t o)", t=PACK))
         res_sb = keep.tile([P, PACK, U], F32, name="res_sb", tag="slot_c", align_bytes=64)
         nc.sync.dma_start(res_sb[:], by_rows(res))
 
+        numer = [keep.tile([P, U], F32, name="numer%d" % t) for t in range(PACK)]
         for t in range(PACK):
             h0 = keep.tile([P, J], F32, name="h0_%d" % t)
             nc.scalar.activation(h0[:], a_banks[t][:], ACT.Tanh)
-            nc.vector.tensor_tensor(page_a[t][:].indirect(offs2_sb[:]), h0[:], gain_wide[t][:], MULT)
+            if t == 0:
+                nc.vector.tensor_tensor(page_a[t][:].indirect(offs2_sb[:]), h0[:], gain_wide[:], MULT)
+            else:
+                h1 = keep.tile([P, J], F32, name="h1_%d" % t)
+                nc.scalar.activation(h1[:], h0[:], ACT.Copy, scale=gain_sb[:, t : t + 1])
+                nc.vector.tensor_copy(page_a[t][:].indirect(offs2_sb[:]), h1[:])
+            nc.gpsimd.tensor_tensor(numer[t][:], page_a[t][:], ground_sb[:, t, :], ADD)
         a_sq = [keep.tile([P, J], F32, name="a_sq%d" % t) for t in range(PACK)]
         for t in range(PACK):
             nc.scalar.activation(a_sq[t][:], a_banks[t][:], ACT.Square)
-        numer = [psum.tile([P, U], F32, name="numer%d" % t) for t in range(PACK)]
 
-        def add_ground(t):
-            turned = psum.tile([P, PACK, P], F32, name="turned%d" % t, tag="bank%d" % t)
-            for b in range(U // P):
-                cols = slice(b * P, (b + 1) * P)
-                nc.tensor.matmul(
-                    turned[:, b, :], ground_sb[:, t, cols], ident[:], start=True, stop=False, is_transpose=True
-                )
-                nc.tensor.matmul(
-                    turned[:, b, :], page_a[t][:, cols], ident[:], start=False, stop=True, is_transpose=True
-                )
-            turned_sb = keep.tile([P, PACK, P], F32, name="turned_sb%d" % t, tag="root%d" % t)
-            nc.scalar.copy(turned_sb[:], turned[:])
-            for b in range(U // P):
-                nc.tensor.transpose(numer[t][:, b * P : (b + 1) * P], turned_sb[:, b, :], ident[:])
-
-        fo_planar = keep.tile([P, PACK, U], BF16, name="fo_planar")
+        chunks = [slice(c0, c0 + CHUNK) for c0 in range(0, U, CHUNK)]
+        pairs = [keep.tile([P, 2, CHUNK, 2], BF16, name="pairs%d" % c) for c in range(len(chunks))]
         wor_bf = keep.tile([P, PACK, P, PACK], BF16, name="wor_bf", align_bytes=64)
         wor_codes = keep.tile([P, F], U32, name="wor_codes", align_bytes=64)
         wor_scales = keep.tile([P, F], U8, name="wor_scales", align_bytes=64)
 
-        def scatter_q(t):
-            root = keep.tile([P, J], F32, name="root%d" % t, tag="root%d" % t)
-            recip = keep.tile([P, J], F32, name="recip%d" % t)
+        def scatter_q(t, recip_tag):
+            root = keep.tile([P, J], F32, name="root%d" % t)
+            recip = keep.tile([P, J], F32, name="recip%d" % t, tag=recip_tag)
             nc.scalar.activation(root[:], a_sq[t][:], ACT.Abs_reciprocal_sqrt, bias=1.0)
             nc.scalar.activation(recip[:], root[:], ACT.Square)
             nc.vector.tensor_copy(page_q[t][:].indirect(offs3_sb[:]), recip[:])
 
-        def outcome(t, cols):
-            nc.vector.scalar_tensor_tensor(
-                fo_planar[:, t, cols], numer[t][:, cols], rs_sb[:, t : t + 1], page_q[t][:, cols], MULT, MULT
-            )
+        def outcome(t):
+            ratio = keep.tile([P, U], F32, name="ratio%d" % t, tag="ratio%d" % t)
+            nc.gpsimd.tensor_tensor(ratio[:], numer[t][:], page_q[t][:], MULT)
+            for c, cols in enumerate(chunks):
+                nc.scalar.activation(pairs[c][:, t // 2, :, t % 2], ratio[:, cols], ACT.Copy, scale=rs_sb[:, t : t + 1])
 
         def round_wor(m0):
             dst, src = dealt_views(wor_bf, wor_raw, m0, m0 + 32)
             nc.scalar.copy(dst, src)
 
-        scatter_q(0)
-        add_ground(0)
-        scatter_q(1)
-        outcome(0, slice(0, U))
-        add_ground(1)
-        round_wor(0)
-        round_wor(32)
-        scatter_q(2)
-        outcome(1, slice(0, U))
-        add_ground(2)
-        round_wor(64)
-        round_wor(96)
+        scatter_q(2, "recip2")
+        scatter_q(0, "recip0")
+        for m0 in range(0, P, 32):
+            round_wor(m0)
         nc.vector.quantize_mx(
             out=wor_codes[:].bitcast(FP8X4), scales=wor_scales[:], in_=wor_bf[:].rearrange("p t m j -> p (t m j)")
         )
-        outcome(2, slice(0, U))
-        scatter_q(3)
-        add_ground(3)
+        scatter_q(1, "recip1")
+        outcome(2)
+        scatter_q(3, "ratio2")
+        outcome(0)
+        outcome(1)
 
         y_codes = keep.tile([P, U], U32, name="y_codes", align_bytes=64)
         y_scales = keep.tile([P, U], U8, name="y_scales", align_bytes=64)
         out_rows = by_rows(out_0)
         out_words = out_1[0].rearrange("p c t -> p (c t)").bitcast(I32)
-        chunks = [slice(c0, c0 + CHUNK) for c0 in range(0, U, CHUNK)]
         y_banks = []
+        last = PACK - 1
         for c, cols in enumerate(chunks):
-            outcome(PACK - 1, cols)
+            nc.vector.scalar_tensor_tensor(
+                pairs[c][:, 1, :, 1], numer[last][:, cols], rs_sb[:, last : last + 1], page_q[last][:, cols], MULT, MULT
+            )
         for c, cols in enumerate(chunks):
             fo_woven = keep.tile([P, CHUNK, PACK], BF16, name="fo_woven%d" % c, align_bytes=64)
-            dst, src = woven_views(fo_woven[:], fo_planar[:, :, cols])
+            dst, src = woven_views(
+                fo_woven[:].bitcast(F32), pairs[c][:].rearrange("p h u e -> p h (u e)").bitcast(F32)
+            )
             nc.scalar.copy(dst, src)
             fo_codes = keep.tile([P, CHUNK], U32, name="fo_codes%d" % c, align_bytes=64)
             fo_scales = keep.tile([P, CHUNK], U8, name="fo_scales%d" % c, align_bytes=64)

@@ -20,6 +20,7 @@ P = 128
 PACK = 4
 QUADS = 4
 CHUNK = 128
+ORDER = (2, 0, 1, 3)
 
 
 def dealt_views(grouped, raw, m0, m1):
@@ -51,7 +52,7 @@ def tile_attend_chpageratio_pl_kernel(
         offs3_sb = lists.tile([P, J // 16], U16, name="offs3_sb")
         tab_bytes = keep.tile([P, T], U8, name="tab_bytes", align_bytes=64)
         nc.vector.memset(tab_bytes[:].bitcast(I32), 0)
-        warm = keep.tile([P, 1], F32, name="warm")
+        warm = keep.tile([P, 1], F32, name="warm", tag="slot_d")
         warm_out = keep.tile([P, 1], F32, name="warm_out")
         nc.vector.memset(warm[:], 0.0)
         nc.sync.dma_start(offs_sb[:], offs)
@@ -68,16 +69,18 @@ def tile_attend_chpageratio_pl_kernel(
         nc.sync.dma_start(tab_sb[:], tab_words[0].rearrange("p c t -> p (c t)").bitcast(I32))
         nc.sync.dma_start(offs2_sb[:], offs2)
         nc.sync.dma_start(offs3_sb[:], offs3)
+        rs_sb = keep.tile([P, PACK], F32, name="rs_sb", tag="slot_d")
+        nc.sync.dma_start(rs_sb[:], rs.rearrange("(p t) o -> p (t o)", t=PACK))
 
         page_a = [keep.tile([P, U], F32, name="page_a%d" % t) for t in range(PACK)]
         page_q = [keep.tile([P, U], F32, name="page_q%d" % t) for t in range(PACK)]
-        for t in range(PACK):
+        for t in ORDER:
             nc.vector.memset(page_a[t][:], 0.0)
-        for t in range(PACK):
+        for t in ORDER:
             nc.vector.memset(page_q[t][:], 1.0)
 
         gain_wide = keep.tile([P, J], F32, name="gain_wide")
-        nc.scalar.copy(gain_wide[:], gain_sb[:, 0:1].to_broadcast([P, J]))
+        nc.scalar.copy(gain_wide[:], gain_sb[:, ORDER[0] : ORDER[0] + 1].to_broadcast([P, J]))
 
         w1_bf = keep.tile([P, PACK, P, PACK], BF16, name="w1_bf", tag="slot_b", align_bytes=64)
         dst, src = dealt_views(w1_bf, w1_raw, 0, 48)
@@ -85,7 +88,7 @@ def tile_attend_chpageratio_pl_kernel(
         dst, src = dealt_views(w1_bf, w1_raw, 48, P)
         nc.vector.tensor_copy(dst, src)
         w1_codes = keep.tile([P, R], U32, name="w1_codes", tag="slot_c", align_bytes=64)
-        w1_scales = keep.tile([P, R], U8, name="w1_scales", tag="slot_d", align_bytes=64)
+        w1_scales = keep.tile([P, R], U8, name="w1_scales", align_bytes=64)
         picked_bytes = keep.tile([P, J], U8, name="picked_bytes", align_bytes=64)
         nc.vector.tensor_copy(picked_bytes[:], tab_bytes[:].indirect(offs_sb[:]))
         nc.vector.quantize_mx(
@@ -94,15 +97,18 @@ def tile_attend_chpageratio_pl_kernel(
         picked_words = keep.tile([P, J], U32, name="picked_words", align_bytes=64)
         nc.vector.tensor_copy(picked_words[:], tab_sb[:].bitcast(U32).indirect(offs_sb[:]))
 
-        a_banks = [psum.tile([P, J], F32, name="a_bank%d" % t, tag="bank%d" % t) for t in range(PACK)]
-        for t in range(PACK):
+        pieces = [(ORDER[0], slice(0, J // 2)), (ORDER[0], slice(J // 2, J))] + [(t, slice(0, J)) for t in ORDER[1:]]
+        a_banks = []
+        for n, (t, slots) in enumerate(pieces):
+            a_bank = psum.tile([P, slots.stop - slots.start], F32, name="a_bank%d" % n, tag="bank%d" % n)
+            a_banks.append(a_bank)
             cols = slice(t * P, (t + 1) * P)
             nc.tensor.matmul_mx(
-                out=a_banks[t][:],
+                out=a_bank[:],
                 lhsT=w1_codes[:, cols].bitcast(FP8X4),
                 lhsT_scale=w1_scales[:, cols],
-                rhs=picked_words[:].bitcast(FP8X4),
-                rhs_scale=picked_bytes[:],
+                rhs=picked_words[:, slots].bitcast(FP8X4),
+                rhs_scale=picked_bytes[:, slots],
                 start=True,
                 stop=True,
             )
@@ -111,111 +117,130 @@ def tile_attend_chpageratio_pl_kernel(
         nc.sync.dma_start(ground_sb[:], by_rows(ground))
         wor_raw = keep.tile([P, PACK, F], F32, name="wor_raw", tag="slot_b", align_bytes=64)
         nc.sync.dma_start(wor_raw[:], by_rows(wor))
-        rs_sb = keep.tile([P, PACK], F32, name="rs_sb", tag="slot_d", align_bytes=64)
-        nc.sync.dma_start(rs_sb[:], rs.rearrange("(p t) o -> p (t o)", t=PACK))
         res_sb = keep.tile([P, PACK, U], F32, name="res_sb", tag="slot_c", align_bytes=64)
         nc.sync.dma_start(res_sb[:], by_rows(res))
 
-        numer = [keep.tile([P, U], F32, name="numer%d" % t) for t in range(PACK)]
-        for t in range(PACK):
-            h0 = keep.tile([P, J], F32, name="h0_%d" % t)
-            nc.scalar.activation(h0[:], a_banks[t][:], ACT.Tanh)
-            if t == 0:
-                nc.vector.tensor_tensor(page_a[t][:].indirect(offs2_sb[:]), h0[:], gain_wide[:], MULT)
+        last = ORDER[-1]
+        numer = {}
+        for n, (t, slots) in enumerate(pieces):
+            width = slots.stop - slots.start
+            h0 = keep.tile([P, width], F32, name="h0_%d" % n)
+            nc.scalar.activation(h0[:], a_banks[n][:], ACT.Tanh)
+            places = page_a[t][:].indirect(offs2_sb[:, slots.start // 16 : slots.stop // 16])
+            if t == ORDER[0]:
+                nc.vector.tensor_tensor(places, h0[:], gain_wide[:, slots], MULT)
             else:
-                h1 = keep.tile([P, J], F32, name="h1_%d" % t)
+                h1 = keep.tile([P, width], F32, name="h1_%d" % n)
                 nc.scalar.activation(h1[:], h0[:], ACT.Copy, scale=gain_sb[:, t : t + 1])
-                nc.vector.tensor_copy(page_a[t][:].indirect(offs2_sb[:]), h1[:])
-            nc.gpsimd.tensor_tensor(numer[t][:], page_a[t][:], ground_sb[:, t, :], ADD)
+                nc.vector.tensor_copy(places, h1[:])
+            if slots.stop == J:
+                numer[t] = keep.tile([P, U], F32, name="numer%d" % t)
+                nc.gpsimd.tensor_tensor(numer[t][:], page_a[t][:], ground_sb[:, t, :], ADD)
         a_sq = [keep.tile([P, J], F32, name="a_sq%d" % t) for t in range(PACK)]
-        for t in range(PACK):
-            nc.scalar.activation(a_sq[t][:], a_banks[t][:], ACT.Square)
+        for n, (t, slots) in enumerate(pieces):
+            nc.scalar.activation(a_sq[t][:, slots], a_banks[n][:], ACT.Square)
 
-        chunks = [slice(c0, c0 + CHUNK) for c0 in range(0, U, CHUNK)]
-        pairs = [keep.tile([P, 2, CHUNK, 2], BF16, name="pairs%d" % c) for c in range(len(chunks))]
+        n_chunks = U // CHUNK
+        chunks = [slice(c * CHUNK, (c + 1) * CHUNK) for c in range(n_chunks)]
+        pairs = keep.tile([P, n_chunks, 2, CHUNK, 2], BF16, name="pairs")
         wor_bf = keep.tile([P, PACK, P, PACK], BF16, name="wor_bf", align_bytes=64)
-        wor_codes = keep.tile([P, F], U32, name="wor_codes", align_bytes=64)
-        wor_scales = keep.tile([P, F], U8, name="wor_scales", align_bytes=64)
+
+        def by_chunks(tile):
+            return tile[:].rearrange("p (c u) -> p c u", u=CHUNK)
 
         def scatter_q(t, recip_tag):
             root = keep.tile([P, J], F32, name="root%d" % t)
-            recip = keep.tile([P, J], F32, name="recip%d" % t, tag=recip_tag)
+            recip = keep.tile([P, J], F32, name="recip%d" % t, tag=recip_tag, align_bytes=64)
             nc.scalar.activation(root[:], a_sq[t][:], ACT.Abs_reciprocal_sqrt, bias=1.0)
             nc.scalar.activation(recip[:], root[:], ACT.Square)
             nc.vector.tensor_copy(page_q[t][:].indirect(offs3_sb[:]), recip[:])
 
-        def outcome(t):
-            ratio = keep.tile([P, U], F32, name="ratio%d" % t, tag="ratio%d" % t)
-            nc.gpsimd.tensor_tensor(ratio[:], numer[t][:], page_q[t][:], MULT)
-            for c, cols in enumerate(chunks):
-                nc.scalar.activation(pairs[c][:, t // 2, :, t % 2], ratio[:, cols], ACT.Copy, scale=rs_sb[:, t : t + 1])
+        for t in ORDER[:-1]:
+            scatter_q(t, "recip%d" % t)
+            scaled = keep.tile([P, U], F32, name="scaled%d" % t, tag="scaled%d" % t, align_bytes=64)
+            nc.scalar.activation(scaled[:], numer[t][:], ACT.Copy, scale=rs_sb[:, t : t + 1])
+            nc.gpsimd.tensor_tensor(pairs[:, :, t // 2, :, t % 2], by_chunks(scaled), by_chunks(page_q[t]), MULT)
 
-        def round_wor(m0):
-            dst, src = dealt_views(wor_bf, wor_raw, m0, m0 + 32)
+        def round_wor(m0, m1):
+            dst, src = dealt_views(wor_bf, wor_raw, m0, m1)
             nc.scalar.copy(dst, src)
 
-        scatter_q(2, "recip2")
-        scatter_q(0, "recip0")
-        for m0 in range(0, P, 32):
-            round_wor(m0)
-        nc.vector.quantize_mx(
-            out=wor_codes[:].bitcast(FP8X4), scales=wor_scales[:], in_=wor_bf[:].rearrange("p t m j -> p (t m j)")
-        )
-        scatter_q(1, "recip1")
-        outcome(2)
-        scatter_q(3, "ratio2")
-        outcome(0)
-        outcome(1)
+        round_wor(0, P // 2)
+        scatter_q(last, "scaled2")
+        round_wor(P // 2, P)
 
+        wor_codes = keep.tile([P, F], U32, name="wor_codes", tag="scaled2", align_bytes=64)
+        wor_scales = keep.tile([P, F], U8, name="wor_scales", align_bytes=64)
         y_codes = keep.tile([P, U], U32, name="y_codes", align_bytes=64)
         y_scales = keep.tile([P, U], U8, name="y_scales", align_bytes=64)
         out_rows = by_rows(out_0)
         out_words = out_1[0].rearrange("p c t -> p (c t)").bitcast(I32)
-        y_banks = []
-        last = PACK - 1
-        for c, cols in enumerate(chunks):
+        fo_codes = [keep.tile([P, CHUNK], U32, name="fo_codes%d" % c, align_bytes=64) for c in range(n_chunks)]
+        fo_scales = [keep.tile([P, CHUNK], U8, name="fo_scales%d" % c, align_bytes=64) for c in range(n_chunks)]
+        y_banks = [psum.tile([P, PACK, CHUNK], F32, name="y_bank%d" % c, tag="bank%d" % c) for c in range(n_chunks)]
+
+        def quantise_fo(c):
+            cols = chunks[c]
             nc.vector.scalar_tensor_tensor(
-                pairs[c][:, 1, :, 1], numer[last][:, cols], rs_sb[:, last : last + 1], page_q[last][:, cols], MULT, MULT
+                pairs[:, c, 1, :, 1], numer[last][:, cols], rs_sb[:, last : last + 1], page_q[last][:, cols], MULT, MULT
             )
-        for c, cols in enumerate(chunks):
             fo_woven = keep.tile([P, CHUNK, PACK], BF16, name="fo_woven%d" % c, align_bytes=64)
-            dst, src = woven_views(
-                fo_woven[:].bitcast(F32), pairs[c][:].rearrange("p h u e -> p h (u e)").bitcast(F32)
-            )
+            dst, src = woven_views(fo_woven[:].bitcast(F32), pairs[:, c].rearrange("p h u e -> p h (u e)").bitcast(F32))
             nc.scalar.copy(dst, src)
-            fo_codes = keep.tile([P, CHUNK], U32, name="fo_codes%d" % c, align_bytes=64)
-            fo_scales = keep.tile([P, CHUNK], U8, name="fo_scales%d" % c, align_bytes=64)
             nc.vector.quantize_mx(
-                out=fo_codes[:].bitcast(FP8X4), scales=fo_scales[:], in_=fo_woven[:].rearrange("p u t -> p (u t)")
+                out=fo_codes[c][:].bitcast(FP8X4), scales=fo_scales[c][:], in_=fo_woven[:].rearrange("p u t -> p (u t)")
             )
-            y_bank = psum.tile([P, PACK, CHUNK], F32, name="y_bank%d" % c, tag="bank%d" % c)
-            y_banks.append(y_bank)
+
+        def quantise_wor(j0, j1):
+            wcols = slice(j0 * P, j1 * P)
+            nc.vector.quantize_mx(
+                out=wor_codes[:, wcols].bitcast(FP8X4),
+                scales=wor_scales[:, wcols],
+                in_=wor_bf[:, j0:j1].rearrange("p t m j -> p (t m j)"),
+            )
+
+        def multiply(c):
             for j in range(PACK):
                 wcols = slice(j * P, (j + 1) * P)
                 nc.tensor.matmul_mx(
-                    out=y_bank[:, j, :],
+                    out=y_banks[c][:, j, :],
                     lhsT=wor_codes[:, wcols].bitcast(FP8X4),
                     lhsT_scale=wor_scales[:, wcols],
-                    rhs=fo_codes[:].bitcast(FP8X4),
-                    rhs_scale=fo_scales[:],
+                    rhs=fo_codes[c][:].bitcast(FP8X4),
+                    rhs_scale=fo_scales[c][:],
                     start=True,
                     stop=True,
                 )
+
+        quantise_fo(0)
+        quantise_wor(0, 2)
+        quantise_wor(2, 4)
+        multiply(0)
+        for c in range(1, n_chunks):
+            quantise_fo(c)
+            multiply(c)
+
+        y_woven = []
         for c, cols in enumerate(chunks):
             y_sb = keep.tile([P, PACK, CHUNK], F32, name="y_sb%d" % c)
-            nc.vector.tensor_tensor(y_sb[:], y_banks[c][:], res_sb[:, :, cols], ADD)
+            parts = [slice(0, CHUNK)] if c < n_chunks - 1 else [slice(0, CHUNK // 2), slice(CHUNK // 2, CHUNK)]
+            for part in parts:
+                span = slice(cols.start + part.start, cols.start + part.stop)
+                nc.vector.tensor_tensor(y_sb[:, :, part], y_banks[c][:, :, part], res_sb[:, :, span], ADD)
+                woven = keep.tile([P, part.stop - part.start, PACK], BF16, name="y_woven%d" % span.start, align_bytes=64)
+                dst, src = woven_views(woven[:], y_sb[:, :, part])
+                nc.scalar.copy(dst, src)
+                y_woven.append((span, woven))
             nc.sync.dma_start(out_rows[:, :, cols], y_sb[:])
-            y_woven = keep.tile([P, CHUNK, PACK], BF16, name="y_woven%d" % c, align_bytes=64)
-            dst, src = woven_views(y_woven[:], y_sb[:])
-            nc.scalar.copy(dst, src)
+        for span, woven in y_woven:
             nc.vector.quantize_mx(
-                out=y_codes[:, cols].bitcast(FP8X4),
-                scales=y_scales[:, cols],
-                in_=y_woven[:].rearrange("p u t -> p (u t)"),
+                out=y_codes[:, span].bitcast(FP8X4),
+                scales=y_scales[:, span],
+                in_=woven[:].rearrange("p u t -> p (u t)"),
             )
-            if c % 2 == 1:
-                half = slice(cols.stop - 2 * CHUNK, cols.stop)
-                nc.sync.dma_start(out_words[:, half], y_codes[:, half].bitcast(I32))
+            if span.stop == U - CHUNK:
+                nc.sync.dma_start(out_words[:, : U - CHUNK], y_codes[:, : U - CHUNK].bitcast(I32))
+        nc.sync.dma_start(out_words[:, U - CHUNK :], y_codes[:, U - CHUNK :].bitcast(I32))
         for q in range(QUADS):
             queue = nc.scalar if q % 2 == 0 else nc.sync
             queue.dma_start(

@@ -19,17 +19,25 @@ ADD = mybir.AluOpType.add
 P = 128
 PACK = 4
 QUADS = 4
+GROUP = 16
 CHUNK = 128
-ORDER = (2, 0, 1, 3)
+ALIGN = 64
+FIRST, LAST = 2, 3
+ORDER = (FIRST, 0, 1, LAST)
+SCALAR_SHARE = 44
 
 
-def dealt_views(grouped, raw, m0, m1):
-    dst = grouped[:].rearrange("p t m j -> p m j t")[:, m0:m1]
+def by_rows(dram):
+    return dram.rearrange("(p t) c -> p t c", t=PACK)
+
+
+def deal_views(rounded, raw, m0, m1):
+    dst = rounded[:].rearrange("p t m j -> p m j t")[:, m0:m1]
     src = raw[:].rearrange("p j (m t) -> p m j t", t=PACK)[:, m0:m1]
     return dst, src
 
 
-def woven_views(woven, planar):
+def weave_views(woven, planar):
     dst = woven.rearrange("p (c i) t -> p c t i", i=PACK)
     src = planar.rearrange("p t (c i) -> p c t i", i=PACK)
     return dst, src
@@ -44,90 +52,98 @@ def tile_attend_chpageratio_pl_kernel(
         keep = ctx.enter_context(tc.tile_pool(name="keep", bufs=1))
         psum = ctx.enter_context(tc.psum_pool(name="psum", bufs=1))
 
-        def by_rows(dram):
-            return dram.rearrange("(p t) c -> p t c", t=PACK)
+        def quantise(codes, scales, values):
+            nc.vector.quantize_mx(out=codes.bitcast(FP8X4), scales=scales, in_=values)
 
-        offs_sb = lists.tile([P, J // 16], U16, name="offs_sb")
-        offs2_sb = lists.tile([P, J // 16], U16, name="offs2_sb")
-        offs3_sb = lists.tile([P, J // 16], U16, name="offs3_sb")
-        tab_bytes = keep.tile([P, T], U8, name="tab_bytes", align_bytes=64)
+        def multiply(out, lhs_codes, lhs_scales, rhs_codes, rhs_scales):
+            nc.tensor.matmul_mx(
+                out=out,
+                lhsT=lhs_codes.bitcast(FP8X4),
+                lhsT_scale=lhs_scales,
+                rhs=rhs_codes.bitcast(FP8X4),
+                rhs_scale=rhs_scales,
+                start=True,
+                stop=True,
+            )
+
+        offs_sb = lists.tile([P, J // GROUP], U16, name="offs_sb")
+        offs2_sb = lists.tile([P, J // GROUP], U16, name="offs2_sb")
+        offs3_sb = lists.tile([P, J // GROUP], U16, name="offs3_sb")
+        tab_bytes = keep.tile([P, T], U8, name="tab_bytes", align_bytes=ALIGN)
         nc.vector.memset(tab_bytes[:].bitcast(I32), 0)
-        warm = keep.tile([P, 1], F32, name="warm", tag="slot_d")
-        warm_out = keep.tile([P, 1], F32, name="warm_out")
-        nc.vector.memset(warm[:], 0.0)
+        zeros = keep.tile([P, J], F32, name="zeros", tag="zeros_then_ground")
+        nc.vector.memset(zeros[:], 0.0)
         nc.sync.dma_start(offs_sb[:], offs)
         gain_sb = keep.tile([P, PACK], F32, name="gain_sb")
         nc.scalar.dma_start(gain_sb[:], gain.rearrange("(p t) o -> p (t o)", t=PACK))
-        w1_raw = keep.tile([P, PACK, R], F32, name="w1_raw", tag="slot_a", align_bytes=64)
+        w1_raw = keep.tile([P, PACK, R], F32, name="w1_raw", tag="w1_then_bytes_then_res", align_bytes=ALIGN)
         nc.sync.dma_start(w1_raw[:], by_rows(w1))
         for q in range(QUADS):
             nc.scalar.dma_start(
                 tab_bytes[32 * q : 32 * q + 4, :].bitcast(I32), tab_scales[0, 4 * q : 4 * q + 4, :].bitcast(I32)
             )
-        nc.scalar.activation(warm_out[:], warm[:], ACT.Tanh)
-        tab_sb = keep.tile([P, T], I32, name="tab_sb", align_bytes=64)
+        tab_sb = keep.tile([P, T], I32, name="tab_sb", tag="tab_then_codes", align_bytes=ALIGN)
         nc.sync.dma_start(tab_sb[:], tab_words[0].rearrange("p c t -> p (c t)").bitcast(I32))
         nc.sync.dma_start(offs2_sb[:], offs2)
         nc.sync.dma_start(offs3_sb[:], offs3)
-        rs_sb = keep.tile([P, PACK], F32, name="rs_sb", tag="slot_d")
-        nc.sync.dma_start(rs_sb[:], rs.rearrange("(p t) o -> p (t o)", t=PACK))
-
-        page_a = [keep.tile([P, U], F32, name="page_a%d" % t) for t in range(PACK)]
-        page_q = [keep.tile([P, U], F32, name="page_q%d" % t) for t in range(PACK)]
-        for t in ORDER:
-            nc.vector.memset(page_a[t][:], 0.0)
-        for t in ORDER:
-            nc.vector.memset(page_q[t][:], 1.0)
 
         gain_wide = keep.tile([P, J], F32, name="gain_wide")
-        nc.scalar.copy(gain_wide[:], gain_sb[:, ORDER[0] : ORDER[0] + 1].to_broadcast([P, J]))
+        nc.scalar.activation(gain_wide[:], zeros[:], ACT.Identity, bias=gain_sb[:, FIRST : FIRST + 1])
+        ground_sb = keep.tile([P, PACK, U], F32, name="ground_sb", tag="zeros_then_ground")
+        nc.sync.dma_start(ground_sb[:], by_rows(ground))
 
-        w1_bf = keep.tile([P, PACK, P, PACK], BF16, name="w1_bf", tag="slot_b", align_bytes=64)
-        dst, src = dealt_views(w1_bf, w1_raw, 0, 48)
-        nc.scalar.copy(dst, src)
-        dst, src = dealt_views(w1_bf, w1_raw, 48, P)
-        nc.vector.tensor_copy(dst, src)
-        w1_codes = keep.tile([P, R], U32, name="w1_codes", tag="slot_c", align_bytes=64)
-        w1_scales = keep.tile([P, R], U8, name="w1_scales", align_bytes=64)
-        picked_bytes = keep.tile([P, J], U8, name="picked_bytes", align_bytes=64)
+        page_h = [keep.tile([P, U], F32, name="page_h%d" % t) for t in range(PACK)]
+        page_inv = [keep.tile([P, U], F32, name="page_inv%d" % t) for t in range(PACK)]
+        for t in ORDER:
+            nc.vector.memset(page_h[t][:], 0.0)
+        for t in ORDER:
+            nc.vector.memset(page_inv[t][:], 1.0)
+
+        w1_bf = keep.tile([P, PACK, P, PACK], BF16, name="w1_bf", tag="w1_bf_then_wor", align_bytes=ALIGN)
+        nc.scalar.copy(*deal_views(w1_bf, w1_raw, 0, SCALAR_SHARE))
+        nc.vector.tensor_copy(*deal_views(w1_bf, w1_raw, SCALAR_SHARE, P))
+
+        w1_scales = keep.tile([P, R], U8, name="w1_scales", align_bytes=ALIGN)
+        w1_codes = {}
+
+        def quantise_w1(t0, t1, codes):
+            quantise(codes, w1_scales[:, t0 * P : t1 * P], w1_bf[:, t0:t1].rearrange("p t m j -> p (t m j)"))
+            for t in range(t0, t1):
+                w1_codes[t] = codes[:, (t - t0) * P : (t - t0 + 1) * P]
+
+        first_codes = keep.tile([P, P], U32, name="first_codes", tag="codes_then_rs", align_bytes=ALIGN)
+        quantise_w1(FIRST, FIRST + 1, first_codes[:])
+        picked_bytes = keep.tile([P, J], U8, name="picked_bytes", tag="w1_then_bytes_then_res", align_bytes=ALIGN)
         nc.vector.tensor_copy(picked_bytes[:], tab_bytes[:].indirect(offs_sb[:]))
-        nc.vector.quantize_mx(
-            out=w1_codes[:].bitcast(FP8X4), scales=w1_scales[:], in_=w1_bf[:].rearrange("p t m j -> p (t m j)")
-        )
-        picked_words = keep.tile([P, J], U32, name="picked_words", align_bytes=64)
+        picked_words = keep.tile([P, J], U32, name="picked_words", align_bytes=ALIGN)
         nc.vector.tensor_copy(picked_words[:], tab_sb[:].bitcast(U32).indirect(offs_sb[:]))
+        other_codes = keep.tile([P, (PACK - 1) * P], U32, name="other_codes", tag="tab_then_codes", align_bytes=ALIGN)
+        quantise_w1(0, FIRST, other_codes[:, : FIRST * P])
+        quantise_w1(LAST, LAST + 1, other_codes[:, FIRST * P :])
 
-        pieces = [(ORDER[0], slice(0, J // 2)), (ORDER[0], slice(J // 2, J))] + [(t, slice(0, J)) for t in ORDER[1:]]
+        pieces = [(FIRST, slice(0, J // 2)), (FIRST, slice(J // 2, J))] + [(t, slice(0, J)) for t in ORDER[1:]]
         a_banks = []
         for n, (t, slots) in enumerate(pieces):
             a_bank = psum.tile([P, slots.stop - slots.start], F32, name="a_bank%d" % n, tag="bank%d" % n)
             a_banks.append(a_bank)
-            cols = slice(t * P, (t + 1) * P)
-            nc.tensor.matmul_mx(
-                out=a_bank[:],
-                lhsT=w1_codes[:, cols].bitcast(FP8X4),
-                lhsT_scale=w1_scales[:, cols],
-                rhs=picked_words[:, slots].bitcast(FP8X4),
-                rhs_scale=picked_bytes[:, slots],
-                start=True,
-                stop=True,
+            multiply(
+                a_bank[:], w1_codes[t], w1_scales[:, t * P : (t + 1) * P], picked_words[:, slots], picked_bytes[:, slots]
             )
 
-        ground_sb = keep.tile([P, PACK, U], F32, name="ground_sb", tag="slot_a", align_bytes=64)
-        nc.sync.dma_start(ground_sb[:], by_rows(ground))
-        wor_raw = keep.tile([P, PACK, F], F32, name="wor_raw", tag="slot_b", align_bytes=64)
+        wor_raw = keep.tile([P, PACK, F], F32, name="wor_raw", tag="w1_bf_then_wor", align_bytes=ALIGN)
         nc.sync.dma_start(wor_raw[:], by_rows(wor))
-        res_sb = keep.tile([P, PACK, U], F32, name="res_sb", tag="slot_c", align_bytes=64)
+        rs_sb = keep.tile([P, PACK], F32, name="rs_sb", tag="codes_then_rs", align_bytes=ALIGN)
+        nc.sync.dma_start(rs_sb[:], rs.rearrange("(p t) o -> p (t o)", t=PACK))
+        res_sb = keep.tile([P, PACK, U], F32, name="res_sb", tag="w1_then_bytes_then_res", align_bytes=ALIGN)
         nc.sync.dma_start(res_sb[:], by_rows(res))
 
-        last = ORDER[-1]
         numer = {}
         for n, (t, slots) in enumerate(pieces):
             width = slots.stop - slots.start
             h0 = keep.tile([P, width], F32, name="h0_%d" % n)
             nc.scalar.activation(h0[:], a_banks[n][:], ACT.Tanh)
-            places = page_a[t][:].indirect(offs2_sb[:, slots.start // 16 : slots.stop // 16])
-            if t == ORDER[0]:
+            places = page_h[t][:].indirect(offs2_sb[:, slots.start // GROUP : slots.stop // GROUP])
+            if t == FIRST:
                 nc.vector.tensor_tensor(places, h0[:], gain_wide[:, slots], MULT)
             else:
                 h1 = keep.tile([P, width], F32, name="h1_%d" % n)
@@ -135,114 +151,95 @@ def tile_attend_chpageratio_pl_kernel(
                 nc.vector.tensor_copy(places, h1[:])
             if slots.stop == J:
                 numer[t] = keep.tile([P, U], F32, name="numer%d" % t)
-                nc.gpsimd.tensor_tensor(numer[t][:], page_a[t][:], ground_sb[:, t, :], ADD)
+                nc.gpsimd.tensor_tensor(numer[t][:], page_h[t][:], ground_sb[:, t, :], ADD)
         a_sq = [keep.tile([P, J], F32, name="a_sq%d" % t) for t in range(PACK)]
         for n, (t, slots) in enumerate(pieces):
             nc.scalar.activation(a_sq[t][:, slots], a_banks[n][:], ACT.Square)
 
         n_chunks = U // CHUNK
         chunks = [slice(c * CHUNK, (c + 1) * CHUNK) for c in range(n_chunks)]
-        pairs = keep.tile([P, n_chunks, 2, CHUNK, 2], BF16, name="pairs")
-        wor_bf = keep.tile([P, PACK, P, PACK], BF16, name="wor_bf", align_bytes=64)
+        fo_pairs = keep.tile([P, n_chunks, 2, CHUNK, 2], BF16, name="fo_pairs")
+        wor_bf = keep.tile([P, PACK, P, PACK], BF16, name="wor_bf", align_bytes=ALIGN)
 
-        def by_chunks(tile):
-            return tile[:].rearrange("p (c u) -> p c u", u=CHUNK)
+        def by_chunks(page):
+            return page[:].rearrange("p (c u) -> p c u", u=CHUNK)
 
-        def scatter_q(t, recip_tag):
+        def scatter_inverse(t, tag):
             root = keep.tile([P, J], F32, name="root%d" % t)
-            recip = keep.tile([P, J], F32, name="recip%d" % t, tag=recip_tag, align_bytes=64)
+            inverse = keep.tile([P, J], F32, name="inverse%d" % t, tag=tag, align_bytes=ALIGN)
             nc.scalar.activation(root[:], a_sq[t][:], ACT.Abs_reciprocal_sqrt, bias=1.0)
-            nc.scalar.activation(recip[:], root[:], ACT.Square)
-            nc.vector.tensor_copy(page_q[t][:].indirect(offs3_sb[:]), recip[:])
+            nc.scalar.activation(inverse[:], root[:], ACT.Square)
+            nc.vector.tensor_copy(page_inv[t][:].indirect(offs3_sb[:]), inverse[:])
 
         for t in ORDER[:-1]:
-            scatter_q(t, "recip%d" % t)
-            scaled = keep.tile([P, U], F32, name="scaled%d" % t, tag="scaled%d" % t, align_bytes=64)
+            scatter_inverse(t, "inverse%d" % t)
+            scaled = keep.tile([P, U], F32, name="scaled%d" % t, tag="scaled%d" % t, align_bytes=ALIGN)
             nc.scalar.activation(scaled[:], numer[t][:], ACT.Copy, scale=rs_sb[:, t : t + 1])
-            nc.gpsimd.tensor_tensor(pairs[:, :, t // 2, :, t % 2], by_chunks(scaled), by_chunks(page_q[t]), MULT)
+            nc.gpsimd.tensor_tensor(fo_pairs[:, :, t // 2, :, t % 2], by_chunks(scaled), by_chunks(page_inv[t]), MULT)
 
-        def round_wor(m0, m1):
-            dst, src = dealt_views(wor_bf, wor_raw, m0, m1)
-            nc.scalar.copy(dst, src)
+        handed_on = "scaled%d" % FIRST
+        nc.scalar.copy(*deal_views(wor_bf, wor_raw, 0, P // 2))
+        scatter_inverse(LAST, handed_on)
+        nc.scalar.copy(*deal_views(wor_bf, wor_raw, P // 2, P))
 
-        round_wor(0, P // 2)
-        scatter_q(last, "scaled2")
-        round_wor(P // 2, P)
-
-        wor_codes = keep.tile([P, F], U32, name="wor_codes", tag="scaled2", align_bytes=64)
-        wor_scales = keep.tile([P, F], U8, name="wor_scales", align_bytes=64)
-        y_codes = keep.tile([P, U], U32, name="y_codes", align_bytes=64)
-        y_scales = keep.tile([P, U], U8, name="y_scales", align_bytes=64)
-        out_rows = by_rows(out_0)
-        out_words = out_1[0].rearrange("p c t -> p (c t)").bitcast(I32)
-        fo_codes = [keep.tile([P, CHUNK], U32, name="fo_codes%d" % c, align_bytes=64) for c in range(n_chunks)]
-        fo_scales = [keep.tile([P, CHUNK], U8, name="fo_scales%d" % c, align_bytes=64) for c in range(n_chunks)]
+        wor_codes = keep.tile([P, F], U32, name="wor_codes", tag=handed_on, align_bytes=ALIGN)
+        wor_scales = keep.tile([P, F], U8, name="wor_scales", align_bytes=ALIGN)
+        y_codes = keep.tile([P, U], U32, name="y_codes", align_bytes=ALIGN)
+        y_scales = keep.tile([P, U], U8, name="y_scales", align_bytes=ALIGN)
+        fo_codes = [keep.tile([P, CHUNK], U32, name="fo_codes%d" % c, align_bytes=ALIGN) for c in range(n_chunks)]
+        fo_scales = [keep.tile([P, CHUNK], U8, name="fo_scales%d" % c, align_bytes=ALIGN) for c in range(n_chunks)]
         y_banks = [psum.tile([P, PACK, CHUNK], F32, name="y_bank%d" % c, tag="bank%d" % c) for c in range(n_chunks)]
+        y_woven = []
 
         def quantise_fo(c):
             cols = chunks[c]
             nc.vector.scalar_tensor_tensor(
-                pairs[:, c, 1, :, 1], numer[last][:, cols], rs_sb[:, last : last + 1], page_q[last][:, cols], MULT, MULT
+                fo_pairs[:, c, LAST // 2, :, LAST % 2],
+                numer[LAST][:, cols],
+                rs_sb[:, LAST : LAST + 1],
+                page_inv[LAST][:, cols],
+                MULT,
+                MULT,
             )
-            fo_woven = keep.tile([P, CHUNK, PACK], BF16, name="fo_woven%d" % c, align_bytes=64)
-            dst, src = woven_views(fo_woven[:].bitcast(F32), pairs[:, c].rearrange("p h u e -> p h (u e)").bitcast(F32))
-            nc.scalar.copy(dst, src)
-            nc.vector.quantize_mx(
-                out=fo_codes[c][:].bitcast(FP8X4), scales=fo_scales[c][:], in_=fo_woven[:].rearrange("p u t -> p (u t)")
-            )
+            fo_woven = keep.tile([P, CHUNK, PACK], BF16, name="fo_woven%d" % c, align_bytes=ALIGN)
+            pair_words = fo_pairs[:, c].rearrange("p h u e -> p h (u e)").bitcast(F32)
+            nc.scalar.copy(*weave_views(fo_woven[:].bitcast(F32), pair_words))
+            quantise(fo_codes[c][:], fo_scales[c][:], fo_woven[:].rearrange("p u t -> p (u t)"))
 
-        def quantise_wor(j0, j1):
-            wcols = slice(j0 * P, j1 * P)
-            nc.vector.quantize_mx(
-                out=wor_codes[:, wcols].bitcast(FP8X4),
-                scales=wor_scales[:, wcols],
-                in_=wor_bf[:, j0:j1].rearrange("p t m j -> p (t m j)"),
-            )
-
-        def multiply(c):
+        def multiply_chunk(c):
             for j in range(PACK):
-                wcols = slice(j * P, (j + 1) * P)
-                nc.tensor.matmul_mx(
-                    out=y_banks[c][:, j, :],
-                    lhsT=wor_codes[:, wcols].bitcast(FP8X4),
-                    lhsT_scale=wor_scales[:, wcols],
-                    rhs=fo_codes[c][:].bitcast(FP8X4),
-                    rhs_scale=fo_scales[c][:],
-                    start=True,
-                    stop=True,
+                f_cols = slice(j * P, (j + 1) * P)
+                multiply(
+                    y_banks[c][:, j, :], wor_codes[:, f_cols], wor_scales[:, f_cols], fo_codes[c][:], fo_scales[c][:]
                 )
 
+        def finish_chunk(c):
+            y_sb = keep.tile([P, PACK, CHUNK], F32, name="y_sb%d" % c)
+            width = CHUNK if c < n_chunks - 1 else CHUNK // 2
+            for u0 in range(0, CHUNK, width):
+                part = slice(u0, u0 + width)
+                span = slice(c * CHUNK + u0, c * CHUNK + u0 + width)
+                nc.vector.tensor_tensor(y_sb[:, :, part], y_banks[c][:, :, part], res_sb[:, :, span], ADD)
+                woven = keep.tile([P, width, PACK], BF16, name="y_woven%d" % span.start, align_bytes=ALIGN)
+                nc.scalar.copy(*weave_views(woven[:], y_sb[:, :, part]))
+                y_woven.append((span, woven))
+            nc.sync.dma_start(by_rows(out_0)[:, :, chunks[c]], y_sb[:])
+
         quantise_fo(0)
-        quantise_wor(0, 2)
-        quantise_wor(2, 4)
-        multiply(0)
+        for j0 in range(0, PACK, 2):
+            f_cols = slice(j0 * P, (j0 + 2) * P)
+            quantise(wor_codes[:, f_cols], wor_scales[:, f_cols], wor_bf[:, j0 : j0 + 2].rearrange("p t m j -> p (t m j)"))
+        multiply_chunk(0)
         for c in range(1, n_chunks):
             quantise_fo(c)
-            multiply(c)
+            multiply_chunk(c)
+            finish_chunk(c - 1)
+        finish_chunk(n_chunks - 1)
 
-        y_woven = []
-        for c, cols in enumerate(chunks):
-            y_sb = keep.tile([P, PACK, CHUNK], F32, name="y_sb%d" % c)
-            parts = [slice(0, CHUNK)] if c < n_chunks - 1 else [slice(0, CHUNK // 2), slice(CHUNK // 2, CHUNK)]
-            for part in parts:
-                span = slice(cols.start + part.start, cols.start + part.stop)
-                nc.vector.tensor_tensor(y_sb[:, :, part], y_banks[c][:, :, part], res_sb[:, :, span], ADD)
-                woven = keep.tile([P, part.stop - part.start, PACK], BF16, name="y_woven%d" % span.start, align_bytes=64)
-                dst, src = woven_views(woven[:], y_sb[:, :, part])
-                nc.scalar.copy(dst, src)
-                y_woven.append((span, woven))
-            nc.sync.dma_start(out_rows[:, :, cols], y_sb[:])
         for span, woven in y_woven:
-            nc.vector.quantize_mx(
-                out=y_codes[:, span].bitcast(FP8X4),
-                scales=y_scales[:, span],
-                in_=woven[:].rearrange("p u t -> p (u t)"),
-            )
-            if span.stop == U - CHUNK:
-                nc.sync.dma_start(out_words[:, : U - CHUNK], y_codes[:, : U - CHUNK].bitcast(I32))
-        nc.sync.dma_start(out_words[:, U - CHUNK :], y_codes[:, U - CHUNK :].bitcast(I32))
+            quantise(y_codes[:, span], y_scales[:, span], woven[:].rearrange("p u t -> p (u t)"))
+        nc.scalar.dma_start(out_1[0].rearrange("p c t -> p (c t)").bitcast(I32), y_codes[:].bitcast(I32))
         for q in range(QUADS):
-            queue = nc.scalar if q % 2 == 0 else nc.sync
-            queue.dma_start(
+            nc.sync.dma_start(
                 out_2[0, 4 * q : 4 * q + 4, :].bitcast(I32), y_scales[32 * q : 32 * q + 4, :].bitcast(I32)
             )

from contextlib import ExitStack

import concourse.mybir as mybir

K, R, F, T, J, U = 512, 512, 512, 2048, 256, 512
FLOPS = 2 * K * R * J + 2 * R * F * U

F32 = mybir.dt.float32
BF16 = mybir.dt.bfloat16
I32 = mybir.dt.int32
U32 = mybir.dt.uint32
U16 = mybir.dt.uint16
U8 = mybir.dt.uint8
FP8X4 = mybir.dt.float8_e4m3fn_x4
ACT = mybir.ActivationFunctionType
MULT = mybir.AluOpType.mult
ADD = mybir.AluOpType.add

P = 128
PACK = 4
QUADS = 4
GROUP = 16
CHUNK = 128
ALIGN = 64
FIRST, LAST = 2, 3
ORDER = (FIRST, 0, 1, LAST)
SCALAR_SHARE = 44


def by_rows(dram):
    return dram.rearrange("(p t) c -> p t c", t=PACK)


def deal_views(rounded, raw, m0, m1):
    dst = rounded[:].rearrange("p t m j -> p m j t")[:, m0:m1]
    src = raw[:].rearrange("p j (m t) -> p m j t", t=PACK)[:, m0:m1]
    return dst, src


def weave_views(woven, planar):
    dst = woven.rearrange("p (c i) t -> p c t i", i=PACK)
    src = planar.rearrange("p t (c i) -> p c t i", i=PACK)
    return dst, src


def tile_attend_chpageratio_pl_kernel(
    tc, tab_words, tab_scales, w1, gain, ground, rs, wor, res, offs, offs2, offs3, out_0, out_1, out_2
):
    nc = tc.nc
    with ExitStack() as ctx:
        lists = ctx.enter_context(tc.tile_pool(name="lists", bufs=1))
        keep = ctx.enter_context(tc.tile_pool(name="keep", bufs=1))
        psum = ctx.enter_context(tc.psum_pool(name="psum", bufs=1))

        def quantise(codes, scales, values):
            nc.vector.quantize_mx(out=codes.bitcast(FP8X4), scales=scales, in_=values)

        def multiply(out, lhs_codes, lhs_scales, rhs_codes, rhs_scales):
            nc.tensor.matmul_mx(
                out=out,
                lhsT=lhs_codes.bitcast(FP8X4),
                lhsT_scale=lhs_scales,
                rhs=rhs_codes.bitcast(FP8X4),
                rhs_scale=rhs_scales,
                start=True,
                stop=True,
            )

        offs_sb = lists.tile([P, J // GROUP], U16, name="offs_sb")
        offs2_sb = lists.tile([P, J // GROUP], U16, name="offs2_sb")
        offs3_sb = lists.tile([P, J // GROUP], U16, name="offs3_sb")
        tab_bytes = keep.tile([P, T], U8, name="tab_bytes", align_bytes=ALIGN)
        nc.vector.memset(tab_bytes[:].bitcast(I32), 0)
        zeros = keep.tile([P, J], F32, name="zeros", tag="zeros_then_ground")
        nc.vector.memset(zeros[:], 0.0)
        nc.sync.dma_start(offs_sb[:], offs)
        gain_sb = keep.tile([P, PACK], F32, name="gain_sb")
        nc.scalar.dma_start(gain_sb[:], gain.rearrange("(p t) o -> p (t o)", t=PACK))
        w1_raw = keep.tile([P, PACK, R], F32, name="w1_raw", tag="w1_then_bytes_then_res", align_bytes=ALIGN)
        nc.sync.dma_start(w1_raw[:], by_rows(w1))
        for q in range(QUADS):
            nc.scalar.dma_start(
                tab_bytes[32 * q : 32 * q + 4, :].bitcast(I32), tab_scales[0, 4 * q : 4 * q + 4, :].bitcast(I32)
            )
        tab_sb = keep.tile([P, T], I32, name="tab_sb", tag="tab_then_codes", align_bytes=ALIGN)
        nc.sync.dma_start(tab_sb[:], tab_words[0].rearrange("p c t -> p (c t)").bitcast(I32))
        nc.sync.dma_start(offs2_sb[:], offs2)
        nc.sync.dma_start(offs3_sb[:], offs3)

        gain_wide = keep.tile([P, J], F32, name="gain_wide")
        nc.scalar.activation(gain_wide[:], zeros[:], ACT.Identity, bias=gain_sb[:, FIRST : FIRST + 1])
        ground_sb = keep.tile([P, PACK, U], F32, name="ground_sb", tag="zeros_then_ground")
        nc.sync.dma_start(ground_sb[:], by_rows(ground))

        page_h = [keep.tile([P, U], F32, name="page_h%d" % t) for t in range(PACK)]
        page_inv = [keep.tile([P, U], F32, name="page_inv%d" % t) for t in range(PACK)]
        for t in ORDER:
            nc.vector.memset(page_h[t][:], 0.0)
        for t in ORDER:
            nc.vector.memset(page_inv[t][:], 1.0)

        w1_bf = keep.tile([P, PACK, P, PACK], BF16, name="w1_bf", tag="w1_bf_then_wor", align_bytes=ALIGN)
        nc.scalar.copy(*deal_views(w1_bf, w1_raw, 0, SCALAR_SHARE))
        nc.vector.tensor_copy(*deal_views(w1_bf, w1_raw, SCALAR_SHARE, P))

        w1_scales = keep.tile([P, R], U8, name="w1_scales", align_bytes=ALIGN)
        w1_codes = {}

        def quantise_w1(t0, t1, codes):
            quantise(codes, w1_scales[:, t0 * P : t1 * P], w1_bf[:, t0:t1].rearrange("p t m j -> p (t m j)"))
            for t in range(t0, t1):
                w1_codes[t] = codes[:, (t - t0) * P : (t - t0 + 1) * P]

        first_codes = keep.tile([P, P], U32, name="first_codes", tag="codes_then_rs", align_bytes=ALIGN)
        quantise_w1(FIRST, FIRST + 1, first_codes[:])
        picked_bytes = keep.tile([P, J], U8, name="picked_bytes", tag="w1_then_bytes_then_res", align_bytes=ALIGN)
        nc.vector.tensor_copy(picked_bytes[:], tab_bytes[:].indirect(offs_sb[:]))
        picked_words = keep.tile([P, J], U32, name="picked_words", align_bytes=ALIGN)
        nc.vector.tensor_copy(picked_words[:], tab_sb[:].bitcast(U32).indirect(offs_sb[:]))
        other_codes = keep.tile([P, (PACK - 1) * P], U32, name="other_codes", tag="tab_then_codes", align_bytes=ALIGN)
        quantise_w1(0, FIRST, other_codes[:, : FIRST * P])
        quantise_w1(LAST, LAST + 1, other_codes[:, FIRST * P :])

        pieces = [(FIRST, slice(0, J // 2)), (FIRST, slice(J // 2, J))] + [(t, slice(0, J)) for t in ORDER[1:]]
        a_banks = []
        for n, (t, slots) in enumerate(pieces):
            a_bank = psum.tile([P, slots.stop - slots.start], F32, name="a_bank%d" % n, tag="bank%d" % n)
            a_banks.append(a_bank)
            multiply(
                a_bank[:], w1_codes[t], w1_scales[:, t * P : (t + 1) * P], picked_words[:, slots], picked_bytes[:, slots]
            )

        wor_raw = keep.tile([P, PACK, F], F32, name="wor_raw", tag="w1_bf_then_wor", align_bytes=ALIGN)
        nc.sync.dma_start(wor_raw[:], by_rows(wor))
        rs_sb = keep.tile([P, PACK], F32, name="rs_sb", tag="codes_then_rs", align_bytes=ALIGN)
        nc.sync.dma_start(rs_sb[:], rs.rearrange("(p t) o -> p (t o)", t=PACK))
        res_sb = keep.tile([P, PACK, U], F32, name="res_sb", tag="w1_then_bytes_then_res", align_bytes=ALIGN)
        nc.sync.dma_start(res_sb[:], by_rows(res))

        numer = {}
        for n, (t, slots) in enumerate(pieces):
            width = slots.stop - slots.start
            h0 = keep.tile([P, width], F32, name="h0_%d" % n)
            nc.scalar.activation(h0[:], a_banks[n][:], ACT.Tanh)
            places = page_h[t][:].indirect(offs2_sb[:, slots.start // GROUP : slots.stop // GROUP])
            if t == FIRST:
                nc.vector.tensor_tensor(places, h0[:], gain_wide[:, slots], MULT)
            else:
                h1 = keep.tile([P, width], F32, name="h1_%d" % n)
                nc.scalar.activation(h1[:], h0[:], ACT.Copy, scale=gain_sb[:, t : t + 1])
                nc.vector.tensor_copy(places, h1[:])
            if slots.stop == J:
                numer[t] = keep.tile([P, U], F32, name="numer%d" % t)
                nc.gpsimd.tensor_tensor(numer[t][:], page_h[t][:], ground_sb[:, t, :], ADD)
        a_sq = [keep.tile([P, J], F32, name="a_sq%d" % t) for t in range(PACK)]
        for n, (t, slots) in enumerate(pieces):
            nc.scalar.activation(a_sq[t][:, slots], a_banks[n][:], ACT.Square)

        n_chunks = U // CHUNK
        chunks = [slice(c * CHUNK, (c + 1) * CHUNK) for c in range(n_chunks)]
        fo_pairs = keep.tile([P, n_chunks, 2, CHUNK, 2], BF16, name="fo_pairs")
        wor_bf = keep.tile([P, PACK, P, PACK], BF16, name="wor_bf", align_bytes=ALIGN)

        def by_chunks(page):
            return page[:].rearrange("p (c u) -> p c u", u=CHUNK)

        def scatter_inverse(t, tag):
            root = keep.tile([P, J], F32, name="root%d" % t)
            inverse = keep.tile([P, J], F32, name="inverse%d" % t, tag=tag, align_bytes=ALIGN)
            nc.scalar.activation(root[:], a_sq[t][:], ACT.Abs_reciprocal_sqrt, bias=1.0)
            nc.scalar.activation(inverse[:], root[:], ACT.Square)
            nc.vector.tensor_copy(page_inv[t][:].indirect(offs3_sb[:]), inverse[:])

        for t in ORDER[:-1]:
            scatter_inverse(t, "inverse%d" % t)
            scaled = keep.tile([P, U], F32, name="scaled%d" % t, tag="scaled%d" % t, align_bytes=ALIGN)
            nc.scalar.activation(scaled[:], numer[t][:], ACT.Copy, scale=rs_sb[:, t : t + 1])
            nc.gpsimd.tensor_tensor(fo_pairs[:, :, t // 2, :, t % 2], by_chunks(scaled), by_chunks(page_inv[t]), MULT)

        handed_on = "scaled%d" % FIRST
        nc.scalar.copy(*deal_views(wor_bf, wor_raw, 0, P // 2))
        scatter_inverse(LAST, handed_on)
        nc.scalar.copy(*deal_views(wor_bf, wor_raw, P // 2, P))

        wor_codes = keep.tile([P, F], U32, name="wor_codes", tag=handed_on, align_bytes=ALIGN)
        wor_scales = keep.tile([P, F], U8, name="wor_scales", align_bytes=ALIGN)
        y_codes = keep.tile([P, U], U32, name="y_codes", align_bytes=ALIGN)
        y_scales = keep.tile([P, U], U8, name="y_scales", align_bytes=ALIGN)
        fo_codes = [keep.tile([P, CHUNK], U32, name="fo_codes%d" % c, align_bytes=ALIGN) for c in range(n_chunks)]
        fo_scales = [keep.tile([P, CHUNK], U8, name="fo_scales%d" % c, align_bytes=ALIGN) for c in range(n_chunks)]
        y_banks = [psum.tile([P, PACK, CHUNK], F32, name="y_bank%d" % c, tag="bank%d" % c) for c in range(n_chunks)]
        y_woven = []

        def quantise_fo(c):
            cols = chunks[c]
            nc.vector.scalar_tensor_tensor(
                fo_pairs[:, c, LAST // 2, :, LAST % 2],
                numer[LAST][:, cols],
                rs_sb[:, LAST : LAST + 1],
                page_inv[LAST][:, cols],
                MULT,
                MULT,
            )
            fo_woven = keep.tile([P, CHUNK, PACK], BF16, name="fo_woven%d" % c, align_bytes=ALIGN)
            pair_words = fo_pairs[:, c].rearrange("p h u e -> p h (u e)").bitcast(F32)
            nc.scalar.copy(*weave_views(fo_woven[:].bitcast(F32), pair_words))
            quantise(fo_codes[c][:], fo_scales[c][:], fo_woven[:].rearrange("p u t -> p (u t)"))

        def multiply_chunk(c):
            for j in range(PACK):
                f_cols = slice(j * P, (j + 1) * P)
                multiply(
                    y_banks[c][:, j, :], wor_codes[:, f_cols], wor_scales[:, f_cols], fo_codes[c][:], fo_scales[c][:]
                )

        def finish_chunk(c):
            y_sb = keep.tile([P, PACK, CHUNK], F32, name="y_sb%d" % c)
            width = CHUNK if c < n_chunks - 1 else CHUNK // 2
            for u0 in range(0, CHUNK, width):
                part = slice(u0, u0 + width)
                span = slice(c * CHUNK + u0, c * CHUNK + u0 + width)
                nc.vector.tensor_tensor(y_sb[:, :, part], y_banks[c][:, :, part], res_sb[:, :, span], ADD)
                woven = keep.tile([P, width, PACK], BF16, name="y_woven%d" % span.start, align_bytes=ALIGN)
                nc.scalar.copy(*weave_views(woven[:], y_sb[:, :, part]))
                y_woven.append((span, woven))
            nc.sync.dma_start(by_rows(out_0)[:, :, chunks[c]], y_sb[:])

        quantise_fo(0)
        for j0 in range(0, PACK, 2):
            f_cols = slice(j0 * P, (j0 + 2) * P)
            quantise(wor_codes[:, f_cols], wor_scales[:, f_cols], wor_bf[:, j0 : j0 + 2].rearrange("p t m j -> p (t m j)"))
        multiply_chunk(0)
        for c in range(1, n_chunks):
            quantise_fo(c)
            multiply_chunk(c)
            finish_chunk(c - 1)
        finish_chunk(n_chunks - 1)

        for span, woven in y_woven:
            quantise(y_codes[:, span], y_scales[:, span], woven[:].rearrange("p u t -> p (u t)"))
        nc.scalar.dma_start(out_1[0].rearrange("p c t -> p (c t)").bitcast(I32), y_codes[:].bitcast(I32))
        for q in range(QUADS):
            nc.sync.dma_start(
                out_2[0, 4 * q : 4 * q + 4, :].bitcast(I32), y_scales[32 * q : 32 * q + 4, :].bitcast(I32)
            )
